import numpy as np, ml_dtypes
CORES = [1,5,73,77,129,133,201,205]
N = 8
G1 = [0,2,4,6]
G2 = [1,3,5,7]
G3 = [0,1,2,3,4,5,6,7]
ROOT3 = 6
def setup_inputs(rng):
    return {"x1": rng.standard_normal((N, 128, 256), dtype=np.float32), "x2": rng.standard_normal((N, 128, 64), dtype=np.float32).astype(ml_dtypes.bfloat16), "x3": rng.standard_normal((N, 128, 2), dtype=np.float32)}
def reference(x1, x2, x3):
    out = {}
    y = np.full((N, 128, 64), np.nan, x1.dtype)
    s = x1[G1].sum(axis=0, dtype=np.float64).astype(x1.dtype)
    for i, r in enumerate(G1):
        y[r] = s[:, 64 * i:64 * i + 64]
    out["y1"] = y
    y = np.full((N, 128, 256), np.nan, x2.dtype)
    s = np.concatenate([x2[r] for r in G2], axis=1)
    for r in G2:
        y[r] = s
    out["y2"] = y
    y = np.full((N, 128, 2), np.nan, x3.dtype)
    for r in G3:
        y[r] = x3[G3[ROOT3]]
    out["y3"] = y
    return out

@@ -1,0 +1,167 @@
+from concourse.bass import DstId, RemoteDMATransfer
+from concourse.mybir import AluOpType
+
+SCRATCH = {
+    "s1": ("dram", [4, 128, 64], "float32"),
+    "r1": ("dram", [2, 128, 64], "float32"),
+    "ag": ("dram", [4, 128, 64], "bfloat16"),
+    "b3": ("dram", [128, 2], "float32"),
+}
+SEMAPHORES = ["ld1", "own1", "gdma", "ld2", "st", "sent", "h1", "r1d", "r1f", "h2", "a2p", "a2x", "a2y", "l3", "a3"]
+
+
+def _eng(lo, n):
+    return ((1 << n) - 1) << lo
+
+
+def _base(c):
+    return c - c % 8
+
+
+def _sides(members, topo, m):
+    par = [topo.chip(c) % 2 for c in members]
+    same = [i for i in range(len(members)) if par[i] == par[m]]
+    cross = [i for i in range(len(members)) if par[i] != par[m]]
+    return same, cross
+
+
+def _fold_core(members, topo, d):
+    same, cross = _sides(members, topo, d)
+    return _base(members[cross[same.index(d)]]) + 2
+
+
+def rank_program(g, core, T, topo):
+    S = T.sem
+    cores = T.cores
+    m1 = [cores[r] for r in T.tables["G1"]]
+    m2 = [cores[r] for r in T.tables["G2"]]
+    m3 = [cores[r] for r in T.tables["G3"]]
+    root = m3[T.tables["ROOT3"]]
+    relay3 = _base(root) + 3
+    direct3 = [c for c in m3 if c != root and topo.may_write(root, c)]
+    across3 = [c for c in m3 if c != root and not topo.may_write(root, c)]
+
+    def did(d):
+        rid, pid = topo.addr(d, core)
+        return DstId(rid=rid, pnc=pid)
+
+    def same_chip(d):
+        return _base(d) == _base(core)
+
+    if core == relay3:
+        g.wait_ge(S.a3, 1)
+        g.remote_dma_fused(
+            [RemoteDMATransfer(dst_ids=[did(c)], dma_engine_mask=_eng(k, 1), remote_sem=S.a3, src=T.b3[:], dst=T.b3[:])
+             for k, c in enumerate(across3)], local_sem=S.sent)
+        g.wait_ge(S.sent, len(across3))
+        return
+
+    for d in range(len(m1)):
+        if core == _fold_core(m1, topo, d):
+            _, cross = _sides(m1, topo, d)
+            g.wait_ge(S.h1, 12)
+            g.remote_dma_fused(
+                [RemoteDMATransfer(dst_ids=[did(m1[d])], dma_engine_mask=_eng(0, 8), remote_sem=S.r1f,
+                                   srcs=[T.s1[s] for s in cross], dsts=[T.r1[1]], alu_op=1)], local_sem=S.sent)
+            g.wait_ge(S.sent, 8)
+            return
+
+    for s in range(len(m2)):
+        _, cross = _sides(m2, topo, s)
+        for k, d in enumerate(cross):
+            if core == _base(m2[s]) + 6 + k:
+                _, back = _sides(m2, topo, d)
+                rid, pid = topo.addr(m2[d], core)
+                g.wait_ge(S.h2, 4)
+                g.remote_dma(T.ag[s], T.ag[s], S.a2x if back.index(s) == 0 else S.a2y, S.sent, pid, rid, _eng(0, 8))
+                g.wait_ge(S.sent, 8)
+                return
+
+    if T.rank_of(core) is None:
+        return
+
+    if core in m1:
+        m = m1.index(core)
+        same, cross = _sides(m1, topo, m)
+        p = [i for i in same if i != m][0]
+        near = [d for d in cross if same_chip(_fold_core(m1, topo, d))][0]
+        far = [d for d in cross if d != near][0]
+
+        def blk(j):
+            return T.x1[:, 64 * j:64 * j + 64]
+
+        if core == root:
+            g.scalar.dma_start(T.b3[:], T.x3[:]).then_inc(S.l3, 16)
+        g.sync.dma_start(T.s1[far], blk(far)).then_inc(S.ld1, 16)
+        g.scalar.dma_start(T.s1[near], blk(near)).then_inc(S.ld1, 16)
+        g.sync.dma_start(T.s1[p], blk(p)).then_inc(S.ld1, 16)
+        g.scalar.dma_start(T.y1[:], blk(m)).then_inc(S.own1, 16)
+        sent = 0
+        if core == root:
+            g.sync.dma_start(T.y3[:], T.x3[:]).then_inc(S.st, 16)
+            g.wait_ge(S.l3, 16)
+            tr = []
+            on, off = 8, 0
+            for c in [relay3] + direct3:
+                if same_chip(c):
+                    e, on = on, on + 1
+                else:
+                    e, off = off, off + 1
+                tr.append(RemoteDMATransfer(dst_ids=[did(c)], dma_engine_mask=_eng(e, 1), remote_sem=S.a3,
+                                            src=T.b3[:], dst=T.b3[:]))
+            g.remote_dma_fused(tr, local_sem=S.sent)
+            sent += len(tr)
+        else:
+            g.sync.wait_ge(S.a3, 1)
+            g.sync.dma_start(T.y3[:], T.b3[:]).then_inc(S.st, 16)
+
+        g.wait_ge(S.ld1, 48)
+        g.remote_dma_fused([
+            RemoteDMATransfer(dst_ids=[did(_fold_core(m1, topo, far))], dma_engine_mask=_eng(0, 4), remote_sem=S.h1,
+                              src=T.s1[far], dst=T.s1[m]),
+            RemoteDMATransfer(dst_ids=[did(m1[p])], dma_engine_mask=_eng(4, 4), remote_sem=S.r1d,
+                              src=T.s1[p], dst=T.r1[0]),
+            RemoteDMATransfer(dst_ids=[did(_fold_core(m1, topo, near))], dma_engine_mask=_eng(8, 8), remote_sem=S.h1,
+                              src=T.s1[near], dst=T.s1[m]),
+        ], local_sem=S.sent)
+        sent += 16
+        g.wait_ge(S.own1, 16)
+        g.wait_ge(S.r1d, 4)
+        g.dma_start(T.y1[:], T.r1[0], accum_op=AluOpType.add, max_dma_last_dim=8192).then_inc(S.gdma, 16)
+        g.wait_ge(S.gdma, 16)
+        g.wait_ge(S.r1f, 8)
+        g.dma_start(T.y1[:], T.r1[1], accum_op=AluOpType.add, max_dma_last_dim=8192).then_inc(S.gdma, 16)
+        g.wait_ge(S.gdma, 32)
+        g.wait_ge(S.sent, sent)
+        g.wait_ge(S.st, 16)
+        return
+
+    m = m2.index(core)
+    same, cross = _sides(m2, topo, m)
+    p = [i for i in same if i != m][0]
+
+    def cols(j):
+        return T.y2[:, 64 * j:64 * j + 64]
+
+    g.sync.dma_start(T.ag[m], T.x2[:]).then_inc(S.ld2, 16)
+    g.scalar.dma_start(cols(m), T.x2[:]).then_inc(S.st, 16)
+    g.wait_ge(S.ld2, 16)
+    g.remote_dma_fused([
+        RemoteDMATransfer(dst_ids=[did(_base(core) + 6)], dma_engine_mask=_eng(8, 4), remote_sem=S.h2,
+                          src=T.ag[m], dst=T.ag[m]),
+        RemoteDMATransfer(dst_ids=[did(_base(core) + 7)], dma_engine_mask=_eng(12, 4), remote_sem=S.h2,
+                          src=T.ag[m], dst=T.ag[m]),
+        RemoteDMATransfer(dst_ids=[did(m2[p])], dma_engine_mask=_eng(0, 8), remote_sem=S.a2p,
+                          src=T.ag[m], dst=T.ag[m]),
+    ], local_sem=S.sent)
+    g.sync.wait_ge(S.a2p, 8)
+    g.sync.dma_start(cols(p), T.ag[p]).then_inc(S.st, 16)
+    g.sync.wait_ge(S.a2x, 8)
+    g.sync.dma_start(cols(cross[0]), T.ag[cross[0]]).then_inc(S.st, 16)
+    g.scalar.wait_ge(S.a2y, 8)
+    g.scalar.dma_start(cols(cross[1]), T.ag[cross[1]]).then_inc(S.st, 16)
+    g.wait_ge(S.a3, 1)
+    g.dma_start(T.y3[:], T.b3[:]).then_inc(S.gdma, 16)
+    g.wait_ge(S.gdma, 16)
+    g.wait_ge(S.sent, 16)
+    g.wait_ge(S.st, 64)

@@ -90,27 +90,14 @@ def rank_program(g, core, T, topo):
         def blk(j):
             return T.x1[:, 64 * j:64 * j + 64]
 
+        g.sync.dma_start(T.s1[far], blk(far)).then_inc(S.ld1, 16)
+        g.scalar.dma_start(T.s1[p], blk(p)).then_inc(S.ld1, 16)
+        g.sync.dma_start(T.s1[near], blk(near)).then_inc(S.ld1, 16)
         if core == root:
             g.scalar.dma_start(T.b3[:], T.x3[:]).then_inc(S.l3, 16)
-        g.sync.dma_start(T.s1[far], blk(far)).then_inc(S.ld1, 16)
-        g.scalar.dma_start(T.s1[near], blk(near)).then_inc(S.ld1, 16)
-        g.sync.dma_start(T.s1[p], blk(p)).then_inc(S.ld1, 16)
         g.scalar.dma_start(T.y1[:], blk(m)).then_inc(S.own1, 16)
-        sent = 0
         if core == root:
             g.sync.dma_start(T.y3[:], T.x3[:]).then_inc(S.st, 16)
-            g.wait_ge(S.l3, 16)
-            tr = []
-            on, off = 8, 0
-            for c in [relay3] + direct3:
-                if same_chip(c):
-                    e, on = on, on + 1
-                else:
-                    e, off = off, off + 1
-                tr.append(RemoteDMATransfer(dst_ids=[did(c)], dma_engine_mask=_eng(e, 1), remote_sem=S.a3,
-                                            src=T.b3[:], dst=T.b3[:]))
-            g.remote_dma_fused(tr, local_sem=S.sent)
-            sent += len(tr)
         else:
             g.sync.wait_ge(S.a3, 1)
             g.sync.dma_start(T.y3[:], T.b3[:]).then_inc(S.st, 16)
@@ -124,7 +111,20 @@ def rank_program(g, core, T, topo):
             RemoteDMATransfer(dst_ids=[did(_fold_core(m1, topo, near))], dma_engine_mask=_eng(8, 8), remote_sem=S.h1,
                               src=T.s1[near], dst=T.s1[m]),
         ], local_sem=S.sent)
-        sent += 16
+        sent = 16
+        if core == root:
+            g.wait_ge(S.l3, 16)
+            tr = []
+            on, off = 8, 0
+            for c in [relay3] + direct3:
+                if same_chip(c):
+                    e, on = on, on + 1
+                else:
+                    e, off = off, off + 1
+                tr.append(RemoteDMATransfer(dst_ids=[did(c)], dma_engine_mask=_eng(e, 1), remote_sem=S.a3,
+                                            src=T.b3[:], dst=T.b3[:]))
+            g.remote_dma_fused(tr, local_sem=S.sent)
+            sent += len(tr)
         g.wait_ge(S.own1, 16)
         g.wait_ge(S.r1d, 4)
         g.dma_start(T.y1[:], T.r1[0], accum_op=AluOpType.add, max_dma_last_dim=8192).then_inc(S.gdma, 16)
@@ -160,8 +160,7 @@ def rank_program(g, core, T, topo):
     g.sync.dma_start(cols(cross[0]), T.ag[cross[0]]).then_inc(S.st, 16)
     g.scalar.wait_ge(S.a2y, 8)
     g.scalar.dma_start(cols(cross[1]), T.ag[cross[1]]).then_inc(S.st, 16)
-    g.wait_ge(S.a3, 1)
-    g.dma_start(T.y3[:], T.b3[:]).then_inc(S.gdma, 16)
-    g.wait_ge(S.gdma, 16)
+    g.scalar.wait_ge(S.a3, 1)
+    g.scalar.dma_start(T.y3[:], T.b3[:]).then_inc(S.st, 16)
     g.wait_ge(S.sent, 16)
-    g.wait_ge(S.st, 64)
+    g.wait_ge(S.st, 80)

from concourse.bass import DstId, RemoteDMATransfer
from concourse.mybir import AluOpType

SCRATCH = {
    "s1": ("dram", [4, 128, 64], "float32"),
    "r1": ("dram", [2, 128, 64], "float32"),
    "ag": ("dram", [4, 128, 64], "bfloat16"),
    "b3": ("dram", [128, 2], "float32"),
}
SEMAPHORES = ["ld1", "own1", "gdma", "ld2", "st", "sent", "h1", "r1d", "r1f", "h2", "a2p", "a2x", "a2y", "l3", "a3"]


def _eng(lo, n):
    return ((1 << n) - 1) << lo


def _base(c):
    return c - c % 8


def _sides(members, topo, m):
    par = [topo.chip(c) % 2 for c in members]
    same = [i for i in range(len(members)) if par[i] == par[m]]
    cross = [i for i in range(len(members)) if par[i] != par[m]]
    return same, cross


def _fold_core(members, topo, d):
    same, cross = _sides(members, topo, d)
    return _base(members[cross[same.index(d)]]) + 2


def rank_program(g, core, T, topo):
    S = T.sem
    cores = T.cores
    m1 = [cores[r] for r in T.tables["G1"]]
    m2 = [cores[r] for r in T.tables["G2"]]
    m3 = [cores[r] for r in T.tables["G3"]]
    root = m3[T.tables["ROOT3"]]
    relay3 = _base(root) + 3
    direct3 = [c for c in m3 if c != root and topo.may_write(root, c)]
    across3 = [c for c in m3 if c != root and not topo.may_write(root, c)]

    def did(d):
        rid, pid = topo.addr(d, core)
        return DstId(rid=rid, pnc=pid)

    def same_chip(d):
        return _base(d) == _base(core)

    if core == relay3:
        g.wait_ge(S.a3, 1)
        g.remote_dma_fused(
            [RemoteDMATransfer(dst_ids=[did(c)], dma_engine_mask=_eng(k, 1), remote_sem=S.a3, src=T.b3[:], dst=T.b3[:])
             for k, c in enumerate(across3)], local_sem=S.sent)
        g.wait_ge(S.sent, len(across3))
        return

    for d in range(len(m1)):
        if core == _fold_core(m1, topo, d):
            _, cross = _sides(m1, topo, d)
            g.wait_ge(S.h1, 12)
            g.remote_dma_fused(
                [RemoteDMATransfer(dst_ids=[did(m1[d])], dma_engine_mask=_eng(0, 8), remote_sem=S.r1f,
                                   srcs=[T.s1[s] for s in cross], dsts=[T.r1[1]], alu_op=1)], local_sem=S.sent)
            g.wait_ge(S.sent, 8)
            return

    for s in range(len(m2)):
        _, cross = _sides(m2, topo, s)
        for k, d in enumerate(cross):
            if core == _base(m2[s]) + 6 + k:
                _, back = _sides(m2, topo, d)
                rid, pid = topo.addr(m2[d], core)
                g.wait_ge(S.h2, 4)
                g.remote_dma(T.ag[s], T.ag[s], S.a2x if back.index(s) == 0 else S.a2y, S.sent, pid, rid, _eng(0, 8))
                g.wait_ge(S.sent, 8)
                return

    if T.rank_of(core) is None:
        return

    if core in m1:
        m = m1.index(core)
        same, cross = _sides(m1, topo, m)
        p = [i for i in same if i != m][0]
        near = [d for d in cross if same_chip(_fold_core(m1, topo, d))][0]
        far = [d for d in cross if d != near][0]

        def blk(j):
            return T.x1[:, 64 * j:64 * j + 64]

        g.sync.dma_start(T.s1[far], blk(far)).then_inc(S.ld1, 16)
        g.scalar.dma_start(T.s1[p], blk(p)).then_inc(S.ld1, 16)
        g.sync.dma_start(T.s1[near], blk(near)).then_inc(S.ld1, 16)
        if core == root:
            g.scalar.dma_start(T.b3[:], T.x3[:]).then_inc(S.l3, 16)
        g.scalar.dma_start(T.y1[:], blk(m)).then_inc(S.own1, 16)
        if core == root:
            g.sync.dma_start(T.y3[:], T.x3[:]).then_inc(S.st, 16)
        else:
            g.sync.wait_ge(S.a3, 1)
            g.sync.dma_start(T.y3[:], T.b3[:]).then_inc(S.st, 16)

        g.wait_ge(S.ld1, 48)
        g.remote_dma_fused([
            RemoteDMATransfer(dst_ids=[did(_fold_core(m1, topo, far))], dma_engine_mask=_eng(0, 4), remote_sem=S.h1,
                              src=T.s1[far], dst=T.s1[m]),
            RemoteDMATransfer(dst_ids=[did(m1[p])], dma_engine_mask=_eng(4, 4), remote_sem=S.r1d,
                              src=T.s1[p], dst=T.r1[0]),
            RemoteDMATransfer(dst_ids=[did(_fold_core(m1, topo, near))], dma_engine_mask=_eng(8, 8), remote_sem=S.h1,
                              src=T.s1[near], dst=T.s1[m]),
        ], local_sem=S.sent)
        sent = 16
        if core == root:
            g.wait_ge(S.l3, 16)
            tr = []
            on, off = 8, 0
            for c in [relay3] + direct3:
                if same_chip(c):
                    e, on = on, on + 1
                else:
                    e, off = off, off + 1
                tr.append(RemoteDMATransfer(dst_ids=[did(c)], dma_engine_mask=_eng(e, 1), remote_sem=S.a3,
                                            src=T.b3[:], dst=T.b3[:]))
            g.remote_dma_fused(tr, local_sem=S.sent)
            sent += len(tr)
        g.wait_ge(S.own1, 16)
        g.wait_ge(S.r1d, 4)
        g.dma_start(T.y1[:], T.r1[0], accum_op=AluOpType.add, max_dma_last_dim=8192).then_inc(S.gdma, 16)
        g.wait_ge(S.gdma, 16)
        g.wait_ge(S.r1f, 8)
        g.dma_start(T.y1[:], T.r1[1], accum_op=AluOpType.add, max_dma_last_dim=8192).then_inc(S.gdma, 16)
        g.wait_ge(S.gdma, 32)
        g.wait_ge(S.sent, sent)
        g.wait_ge(S.st, 16)
        return

    m = m2.index(core)
    same, cross = _sides(m2, topo, m)
    p = [i for i in same if i != m][0]

    def cols(j):
        return T.y2[:, 64 * j:64 * j + 64]

    g.sync.dma_start(T.ag[m], T.x2[:]).then_inc(S.ld2, 16)
    g.scalar.dma_start(cols(m), T.x2[:]).then_inc(S.st, 16)
    g.wait_ge(S.ld2, 16)
    g.remote_dma_fused([
        RemoteDMATransfer(dst_ids=[did(_base(core) + 6)], dma_engine_mask=_eng(8, 4), remote_sem=S.h2,
                          src=T.ag[m], dst=T.ag[m]),
        RemoteDMATransfer(dst_ids=[did(_base(core) + 7)], dma_engine_mask=_eng(12, 4), remote_sem=S.h2,
                          src=T.ag[m], dst=T.ag[m]),
        RemoteDMATransfer(dst_ids=[did(m2[p])], dma_engine_mask=_eng(0, 8), remote_sem=S.a2p,
                          src=T.ag[m], dst=T.ag[m]),
    ], local_sem=S.sent)
    g.sync.wait_ge(S.a2p, 8)
    g.sync.dma_start(cols(p), T.ag[p]).then_inc(S.st, 16)
    g.sync.wait_ge(S.a2x, 8)
    g.sync.dma_start(cols(cross[0]), T.ag[cross[0]]).then_inc(S.st, 16)
    g.scalar.wait_ge(S.a2y, 8)
    g.scalar.dma_start(cols(cross[1]), T.ag[cross[1]]).then_inc(S.st, 16)
    g.scalar.wait_ge(S.a3, 1)
    g.scalar.dma_start(T.y3[:], T.b3[:]).then_inc(S.st, 16)
    g.wait_ge(S.sent, 16)
    g.wait_ge(S.st, 80)
